import numpy as np
import ml_dtypes


def mxq(x, axis, fmt="e4m3"):
    dtype, down = {"e4m3": (ml_dtypes.float8_e4m3fn, 7), "e5m2": (ml_dtypes.float8_e5m2, 14)}[fmt]
    v = np.moveaxis(np.asarray(x, np.float32).astype(ml_dtypes.bfloat16).astype(np.float64), axis, -1)
    blocks = v.reshape(v.shape[:-1] + (-1, 32))
    amax = np.abs(blocks).max(-1, keepdims=True)
    byte = np.maximum(np.where(amax > 0, np.frexp(amax)[1] - 1 + 127, 0) - down, 1)
    scale = np.exp2(byte - 127.0)
    codes = (blocks / scale).astype(np.float32).astype(dtype).astype(np.float64)
    return np.moveaxis((codes * scale).reshape(v.shape), -1, axis)


WIDE = False


def mx_kscale(k):
    if not WIDE:
        return np.ones(k)
    levels = np.array([10, -10, 5, -5, 0])
    if k % 512:
        return np.exp2(np.random.permutation(np.resize(levels, k // 32))).repeat(32)
    a = np.empty((k // 512, 16))
    for p in range(k // 512):
        a[p, :8] = np.random.permutation(np.resize(levels, 8))
        for g in range(8):
            far = levels[np.abs(levels - a[p, g]) >= 10]
            a[p, g + 8] = far[np.random.randint(len(far))]
    return np.exp2(a.ravel()).repeat(32)


def f64(x):
    return np.asarray(x).astype(np.float64)


def striped(idx):
    return np.tile(idx.reshape(-1, 16).T, (8, 1)).astype(np.uint16)


def unstriped(offs):
    return offs[:16].T.reshape(-1).astype(np.int64)


def striped8(idx):
    return np.concatenate([x.reshape(-1, 16).T for x in idx]).astype(np.uint16)


def runs(offs, k):
    lists = np.stack([offs[16 * r : 16 * r + 16].T.reshape(-1) for r in range(8)]).astype(np.int64)
    return lists[np.arange(k) % 512 // 64]


def pack_weight(w):
    k, n = w.shape
    w = f64(np.asarray(w, np.float32).astype(ml_dtypes.bfloat16)).reshape(k // 32, 32, n)
    amax = np.abs(w).max(1)
    byte = np.clip(np.where(amax > 0, np.frexp(amax)[1] - 1 + 127 - 7, 1), 1, 254)
    scaled = (w * np.exp2(127.0 - byte)[:, None, :]).reshape(k, n).astype(np.float32)
    words = np.ascontiguousarray(scaled.reshape(k // 512, 128, 4, n).transpose(0, 1, 3, 2)).astype(ml_dtypes.float8_e4m3fn).view(np.uint8)
    return words, np.ascontiguousarray(byte.astype(np.uint8).reshape(k // 512, 16, n))


def unpack_weight(words, scales):
    g, p, n, _ = words.shape
    vals = np.ascontiguousarray(words).view(ml_dtypes.float8_e4m3fn).astype(np.float64) * np.repeat(np.exp2(scales.astype(np.float64) - 127.0), 8, axis=1)[..., None]
    return vals.transpose(0, 1, 3, 2).reshape(g * 512, n)


E2M1 = np.array([0.0, 0.5, 1.0, 1.5, 2.0, 3.0, 4.0, 6.0, -0.0, -0.5, -1.0, -1.5, -2.0, -3.0, -4.0, -6.0])


def pack_fp4(w):
    k, n = w.shape
    w = f64(np.asarray(w, np.float32).astype(ml_dtypes.bfloat16)).reshape(k // 32, 32, n)
    amax = np.abs(w).max(1)
    mant, ex = np.frexp(amax / 6.0)
    byte = np.clip(np.where(amax > 0, np.where(mant > 0.5, ex, ex - 1) + 127, 1), 1, 254)
    scaled = (w * np.exp2(127.0 - byte)[:, None, :]).reshape(k, n).astype(np.float32)
    c = np.ascontiguousarray(scaled.reshape(k // 512, 128, 4, n).transpose(0, 1, 3, 2)).astype(ml_dtypes.float4_e2m1fn).view(np.uint8) & 0xF
    words = (c[..., 0::2] | (c[..., 1::2] << 4)).reshape(k // 512, 128, 2 * n)
    return np.ascontiguousarray(words), np.ascontiguousarray(byte.astype(np.uint8).reshape(k // 512, 16, n))


def unpack_fp4(words, scales):
    g, _, n = scales.shape
    words = np.ascontiguousarray(words).reshape(g, 128, n, 2)
    nib = np.empty((g, 128, n, 4), np.uint8)
    nib[..., 0::2] = words & 0xF
    nib[..., 1::2] = words >> 4
    vals = E2M1[nib] * np.repeat(np.exp2(scales.astype(np.float64) - 127.0), 8, axis=1)[..., None]
    return vals.transpose(0, 1, 3, 2).reshape(g * 512, n)


def sigmoid(v):
    return 1.0 / (1.0 + np.exp(-np.maximum(v, -700.0)))

def planes(y):
    n, m = y.shape
    v = y.astype(np.float32).astype(ml_dtypes.bfloat16).astype(np.float64).reshape(n // 32, 32, m)
    top = np.abs(v).max(1)
    byte = np.clip(np.where(top > 0, np.frexp(top)[1] - 1 + 127 - 7, 1), 1, 254)
    codes = (v * np.exp2(127.0 - byte)[:, None, :]).reshape(n, m).astype(np.float32).astype(ml_dtypes.float8_e4m3fn).view(np.uint8)
    words = codes.reshape(n // 512, 128, 4, m).transpose(0, 1, 3, 2)
    return np.ascontiguousarray(words), np.ascontiguousarray(byte.astype(np.uint8).reshape(n // 512, 16, m))


K, T, S, H, C = 512, 2048, 512, 512, 512


def setup_inputs():
    n = np.random.standard_normal
    s = mx_kscale(K)[:, None]
    packed_xT = pack_weight(n((K, T)) * s)
    packed_w1 = pack_fp4(n((K, H)) / np.sqrt(K) / s)
    packed_w2 = pack_fp4(n((K, H)) / np.sqrt(K) / s)
    return {
        "x_words": packed_xT[0],
        "x_scales": packed_xT[1],
        "w1_words": packed_w1[0],
        "w1_scales": packed_w1[1],
        "w2_words": packed_w2[0],
        "w2_scales": packed_w2[1],
        "gs": (np.random.uniform(0.5, 1.5, (K, 1)) / s).astype(np.float32),
        "offs": striped(np.random.permutation(T)[:S]),
        "two": striped(np.random.permutation(T)[:S]),
        "n1": striped8(np.stack([np.random.permutation(S) for _ in range(8)])),
        "n2": striped8(np.stack([np.random.permutation(S) for _ in range(8)])),
        "cand": striped(np.random.permutation(T)[:C]),
        "n3": striped8(np.stack([np.random.permutation(S) for _ in range(8)])),
        "n4": striped8(np.stack([np.random.permutation(S) for _ in range(8)])),
    }


def reference(x_words, x_scales, w1_words, w1_scales, w2_words, w2_scales, gs, offs, two, n1, n2, cand, n3, n4):
    x_cand = unpack_weight(x_words, x_scales)[:, unstriped(cand)]
    xq = unpack_weight(x_words, x_scales)[:, unstriped(offs)]
    y = unpack_fp4(w1_words, w1_scales).T @ xq
    x_two = unpack_weight(x_words, x_scales)[:, unstriped(two)]
    d = unpack_fp4(w2_words, w2_scales).T @ x_two
    z = f64(gs) * (y * (sigmoid(d[np.arange(H)[:, None], runs(n2, H)])) - (0.5 * (y[np.arange(H)[:, None], runs(n1, H)])))
    s = 0.0625 * ((x_cand.T @ mxq(z, 0, "e4m3")))
    sm = np.maximum(s, s[np.arange(C)[:, None], runs(n4, C)])
    ds = np.zeros((C, S))
    ds[np.arange(C)[:, None], runs(n3, C)] = sm
    out_0 = ds * sigmoid(s)
    return (out_0,) + planes(out_0)

@@ -1,0 +1,256 @@
+from contextlib import ExitStack
+
+import concourse.mybir as mybir
+
+K, T, S, H, C = 512, 2048, 512, 512, 512
+FLOPS = 3 * 2 * 512 * 512 * 512
+
+F32 = mybir.dt.float32
+BF16 = mybir.dt.bfloat16
+I32 = mybir.dt.int32
+U32 = mybir.dt.uint32
+U16 = mybir.dt.uint16
+U8 = mybir.dt.uint8
+FP8X4 = mybir.dt.float8_e4m3fn_x4
+FP4X4 = mybir.dt.float4_e2m1fn_x4
+ALU = mybir.AluOpType
+ACT = mybir.ActivationFunctionType
+
+P = 128
+PACK = 4
+WINDOW = 1024
+HALF = 256
+
+
+def tile_picked_twcgatebsendg_none_po_kernel(
+    tc, x_words, x_scales, w1_words, w1_scales, w2_words, w2_scales, gs, offs, two, n1, n2, cand, n3, n4, out_0, out_1, out_2
+):
+    nc = tc.nc
+    with ExitStack() as ctx:
+        keep = ctx.enter_context(tc.tile_pool(name="keep", bufs=1))
+        psum = ctx.enter_context(tc.psum_pool(name="psum", bufs=1))
+
+        def load_list(name, src):
+            t = keep.tile([P, S // 16], U16, name=name)
+            nc.sync.dma_start(t[:], src)
+            return t
+
+        def load_scale_rows(queue, dst, src):
+            for q in range(4):
+                queue.dma_start(dst[32 * q : 32 * q + 4, :].bitcast(I32), src[0, 4 * q : 4 * q + 4, :].bitcast(I32))
+
+        xs = keep.tile([P, T], U8, name="xs", align_bytes=64)
+        ws2_raw = keep.tile([P, H], U8, name="ws2_raw", tag="slot_a", align_bytes=64)
+        ws1_raw = keep.tile([P, H], U8, name="ws1_raw", tag="slot_b", align_bytes=64)
+        nc.vector.memset(xs[:].bitcast(I32), 0)
+        nc.vector.memset(ws2_raw[:].bitcast(I32), 0)
+        nc.vector.memset(ws1_raw[:].bitcast(I32), 0)
+
+        w2_raw = keep.tile([P, 2 * H], U8, name="w2_raw", align_bytes=64)
+        w1_raw = keep.tile([P, 2 * H], U8, name="w1_raw", align_bytes=64)
+        xw = keep.tile([P, T], I32, name="xw", align_bytes=64)
+        gs_t = keep.tile([P, PACK], F32, name="gs_t")
+        nc.sync.dma_start(w2_raw[:].bitcast(I32), w2_words[0].bitcast(I32))
+        nc.sync.dma_start(w1_raw[:].bitcast(I32), w1_words[0].bitcast(I32))
+        two_t = load_list("two_t", two)
+        offs_t = load_list("offs_t", offs)
+        load_scale_rows(nc.sync, xs, x_scales)
+        nc.sync.dma_start(xw[:], x_words[0].rearrange("p n t -> p (n t)").bitcast(I32))
+        load_scale_rows(nc.sync, ws2_raw, w2_scales)
+        cand_t = load_list("cand_t", cand)
+        load_scale_rows(nc.sync, ws1_raw, w1_scales)
+        nc.sync.dma_start(gs_t[:], gs.rearrange("(p t) o -> p (t o)", t=PACK))
+        n2_t = load_list("n2_t", n2)
+        n1_t = load_list("n1_t", n1)
+        n4_t = load_list("n4_t", n4)
+        n3_t = load_list("n3_t", n3)
+
+        def deal_fp4_words(name, raw):
+            d = keep.tile([P, 2 * H], U8, name=name, align_bytes=64)
+            nc.vector.tensor_copy(d[:].rearrange("p (t m b) -> p t m b", t=PACK, b=2), raw[:].rearrange("p (m t b) -> p t m b", t=PACK, b=2))
+            return d
+
+        def deal(name, raw, dtype):
+            d = keep.tile([P, S], dtype, name=name, align_bytes=64)
+            nc.vector.tensor_copy(d[:].rearrange("p (t m) -> p t m", t=PACK), raw[:].rearrange("p (m t) -> p t m", t=PACK))
+            return d
+
+        def gather_words(name, lst, slot):
+            g = keep.tile([P, S], I32, name=name, tag=slot, align_bytes=64)
+            nc.vector.tensor_copy(g[:].bitcast(U32), xw[:].bitcast(U32).indirect(lst[:]))
+            return g
+
+        def gather_bytes(name, lst):
+            g = keep.tile([P, S], U8, name=name, align_bytes=64)
+            nc.vector.tensor_copy(g[:], xs[:].indirect(lst[:]))
+            return g
+
+        w2 = deal_fp4_words("w2", w2_raw)
+        w1 = deal_fp4_words("w1", w1_raw)
+        two_s = gather_bytes("two_s", two_t)
+        two_w = gather_words("two_w", two_t, "slot_c")
+        ws2 = deal("ws2", ws2_raw, U8)
+        offs_s = gather_bytes("offs_s", offs_t)
+        offs_w = gather_words("offs_w", offs_t, "slot_a")
+        ws1 = deal("ws1", ws1_raw, U8)
+        half_gs = keep.tile([P, PACK], F32, name="half_gs")
+        nc.vector.tensor_scalar(half_gs[:], gs_t[:], -0.5, None, ALU.mult)
+        cand_s_raw = gather_bytes("cand_s_raw", cand_t)
+        cand_w_raw = gather_words("cand_w_raw", cand_t, "slot_b")
+        cand_s = deal("cand_s", cand_s_raw, U8)
+        cand_w = deal("cand_w", cand_w_raw, I32)
+
+        def project(bank, w, ws, xg, xgs, t):
+            acc = psum.tile([P, S], F32, name="acc", tag="bank%d" % bank)
+            nc.tensor.matmul_mx(
+                out=acc[:],
+                lhsT=w[:, 2 * P * t : 2 * P * (t + 1)].bitcast(FP4X4),
+                lhsT_scale=ws[:, P * t : P * (t + 1)],
+                rhs=xg[:].bitcast(FP8X4),
+                rhs_scale=xgs[:],
+                start=True,
+                stop=True,
+            )
+            return acc
+
+        d_ps = [project(t, w2, ws2, two_w, two_s, t) for t in range(PACK)]
+        y_ps = [project(PACK + t, w1, ws1, offs_w, offs_s, t) for t in range(PACK)]
+
+        def lay_pair(copy, dst, src, cols, pair):
+            copy(
+                dst[:, cols, 2 * pair : 2 * pair + 2].rearrange("p (c i) t -> p c t i", i=4),
+                src[pair][:, :, cols].rearrange("p t (c i) -> p c t i", i=4),
+            )
+
+        def interleave(dst, src, cols):
+            lay_pair(nc.scalar.copy if cols.start == 0 else nc.vector.tensor_copy, dst, src, cols, 1)
+
+        whole = slice(0, S)
+        halves = [slice(0, HALF), slice(HALF, S)]
+        z_bf = keep.tile([P, S, PACK], BF16, name="z_bf", align_bytes=64)
+        z_codes = keep.tile([P, S], I32, name="z_codes", align_bytes=64)
+        z_scales = keep.tile([P, S], U8, name="z_scales", align_bytes=64)
+        z = [keep.tile([P, 2, S], F32, name="z%d" % u) for u in range(2)]
+        d_win = [keep.tile([P, WINDOW], F32, name="d_win%d" % t) for t in range(PACK)]
+        h_win = [keep.tile([P, WINDOW], F32, name="h_win%d" % t) for t in range(PACK)]
+        gated = [keep.tile([P, S], F32, name="gated%d" % t) for t in range(PACK)]
+        other = [keep.tile([P, S], F32, name="other%d" % t) for t in range(PACK)]
+
+        def look(lst, cols):
+            return lst[:, cols.start // 16 : cols.stop // 16]
+
+        def gate_on_scalar(t):
+            nc.scalar.copy(d_win[t][:, :S], d_ps[t][:])
+            nc.scalar.activation(other[t][:], d_win[t][:].indirect(n2_t[:]), ACT.Sigmoid)
+
+        def half_y(t):
+            nc.scalar.activation(h_win[t][:, :S], y_ps[t][:], ACT.Copy, scale=half_gs[:, t : t + 1])
+
+        def apply_gate(t, cols):
+            nc.vector.scalar_tensor_tensor(gated[t][:, cols], y_ps[t][:, cols], gs_t[:, t : t + 1], other[t][:, cols], ALU.mult, ALU.mult)
+
+        def mix(t, cols):
+            nc.vector.tensor_tensor(z[t // 2][:, t % 2, cols], h_win[t][:].indirect(look(n1_t, cols)), gated[t][:, cols], ALU.add)
+
+        nc.scalar.activation(d_win[0][:, :S], d_ps[0][:], ACT.Sigmoid)
+        gate_on_scalar(1)
+        nc.scalar.activation(other[0][:], y_ps[0][:], ACT.Copy, scale=gs_t[:, 0:1])
+        half_y(0)
+        half_y(1)
+        gate_on_scalar(2)
+        half_y(2)
+        gate_on_scalar(3)
+        half_y(3)
+        nc.vector.tensor_tensor(gated[0][:], d_win[0][:].indirect(n2_t[:]), other[0][:], ALU.mult)
+        apply_gate(1, whole)
+        mix(0, whole)
+        apply_gate(2, whole)
+        mix(1, whole)
+        mix(2, whole)
+        for cols in halves:
+            apply_gate(3, cols)
+        for cols in halves:
+            mix(3, cols)
+        lay_pair(nc.scalar.copy, z_bf, z, whole, 0)
+
+        for cols in halves:
+            interleave(z_bf, z, cols)
+        for cols in reversed(halves):
+            nc.vector.quantize_mx(out=z_codes[:, cols].bitcast(FP8X4), scales=z_scales[:, cols], in_=z_bf[:, cols, :].rearrange("p c t -> p (c t)"))
+
+        s_win = [keep.tile([P, WINDOW], F32, name="s_win%d" % t) for t in range(PACK)]
+        s_own = [keep.tile([P, S], F32, name="s_own%d" % t) for t in range(PACK)]
+        sig = [keep.tile([P, S], F32, name="sig%d" % t) for t in range(PACK)]
+        rise = [keep.tile([P, S], F32, name="rise%d" % t) for t in range(PACK)]
+        lift = [keep.tile([P, S], F32, name="lift%d" % t) for t in range(PACK)]
+        ds = [keep.tile([P, WINDOW], F32, name="ds%d" % t) for t in range(PACK)]
+        o = [keep.tile([P, 2, S], F32, name="o%d" % u) for u in range(2)]
+        o_bf = keep.tile([P, S, PACK], BF16, name="o_bf", align_bytes=64)
+        out_rows = out_0.rearrange("(p t) j -> p t j", t=PACK)
+        s_ps = {}
+
+        def pieces(t):
+            return [halves[1], halves[0]] if t == 0 else [whole]
+
+        def score(t):
+            for u, cols in enumerate(pieces(t)):
+                acc = psum.tile([P, cols.stop - cols.start], F32, name="acc", tag="bank%d" % (t + PACK * u))
+                nc.tensor.matmul_mx(
+                    out=acc[:],
+                    lhsT=cand_w[:, P * t : P * (t + 1)].bitcast(FP8X4),
+                    lhsT_scale=cand_s[:, P * t : P * (t + 1)],
+                    rhs=z_codes[:, cols].bitcast(FP8X4),
+                    rhs_scale=z_scales[:, cols],
+                    start=True,
+                    stop=True,
+                )
+                s_ps[t, u] = acc
+
+        def fetch(t):
+            for u, cols in enumerate(pieces(t)):
+                nc.scalar.activation(s_win[t][:, cols], s_ps[t, u][:], ACT.Copy, scale=0.0625)
+                nc.scalar.activation(s_own[t][:, cols], s_ps[t, u][:], ACT.Copy, scale=0.0625)
+            for cols in pieces(t):
+                nc.vector.tensor_tensor(rise[t][:, cols], s_win[t][:].indirect(n4_t[:, cols.start // 16 : cols.stop // 16]), s_own[t][:, cols], ALU.subtract)
+
+        def gate(t):
+            nc.scalar.activation(sig[t][:], s_own[t][:], ACT.Sigmoid)
+
+        def send(t):
+            nc.scalar.activation(lift[t][:], rise[t][:], ACT.Relu)
+            nc.vector.tensor_tensor(ds[t][:].indirect(n3_t[:]), lift[t][:], s_own[t][:], ALU.add)
+
+        def finish(t, cols):
+            nc.vector.tensor_tensor(o[t // 2][:, t % 2, cols], ds[t][:, cols], sig[t][:, cols], ALU.mult)
+            nc.sync.dma_start(out_rows[:, t, cols], o[t // 2][:, t % 2, cols])
+
+        for t in range(PACK):
+            score(t)
+        for t in range(PACK):
+            fetch(t)
+        send(0)
+        send(1)
+        gate(0)
+        finish(0, whole)
+        send(2)
+        gate(1)
+        finish(1, whole)
+        gate(2)
+        finish(2, whole)
+        send(3)
+        gate(3)
+        lay_pair(nc.scalar.copy, o_bf, o, whole, 0)
+        for cols in halves:
+            finish(3, cols)
+
+        o_codes = keep.tile([P, S], I32, name="o_codes", align_bytes=64)
+        o_scales = keep.tile([P, S], U8, name="o_scales", align_bytes=64)
+        for cols in halves:
+            interleave(o_bf, o, cols)
+        words_out = out_1[0].rearrange("p n t -> p (n t)").bitcast(I32)
+        for cols in reversed(halves):
+            nc.vector.quantize_mx(out=o_codes[:, cols].bitcast(FP8X4), scales=o_scales[:, cols], in_=o_bf[:, cols, :].rearrange("p c t -> p (c t)"))
+            nc.scalar.dma_start(words_out[:, cols], o_codes[:, cols])
+        for q in range(4):
+            eng = nc.sync if q % 2 == 0 else nc.scalar
+            eng.dma_start(out_2[0, 4 * q : 4 * q + 4, :].bitcast(I32), o_scales[32 * q : 32 * q + 4, :].bitcast(I32))

@@ -46,6 +46,11 @@ def tile_picked_twcgatebsendg_none_po_kernel(
         nc.vector.memset(ws2_raw[:].bitcast(I32), 0)
         nc.vector.memset(ws1_raw[:].bitcast(I32), 0)
 
+        warm_in = keep.tile([P, 1], F32, name="warm_in")
+        warm_out = keep.tile([P, 1], F32, name="warm_out")
+        nc.gpsimd.memset(warm_in[:], 0.0)
+        nc.scalar.activation(warm_out[:], warm_in[:], ACT.Sigmoid)
+
         w2_raw = keep.tile([P, 2 * H], U8, name="w2_raw", align_bytes=64)
         w1_raw = keep.tile([P, 2 * H], U8, name="w1_raw", align_bytes=64)
         xw = keep.tile([P, T], I32, name="xw", align_bytes=64)
@@ -58,9 +63,9 @@ def tile_picked_twcgatebsendg_none_po_kernel(
         nc.sync.dma_start(xw[:], x_words[0].rearrange("p n t -> p (n t)").bitcast(I32))
         load_scale_rows(nc.sync, ws2_raw, w2_scales)
         cand_t = load_list("cand_t", cand)
+        n2_t = load_list("n2_t", n2)
         load_scale_rows(nc.sync, ws1_raw, w1_scales)
         nc.sync.dma_start(gs_t[:], gs.rearrange("(p t) o -> p (t o)", t=PACK))
-        n2_t = load_list("n2_t", n2)
         n1_t = load_list("n1_t", n1)
         n4_t = load_list("n4_t", n4)
         n3_t = load_list("n3_t", n3)
@@ -93,8 +98,9 @@ def tile_picked_twcgatebsendg_none_po_kernel(
         offs_s = gather_bytes("offs_s", offs_t)
         offs_w = gather_words("offs_w", offs_t, "slot_a")
         ws1 = deal("ws1", ws1_raw, U8)
-        half_gs = keep.tile([P, PACK], F32, name="half_gs")
-        nc.vector.tensor_scalar(half_gs[:], gs_t[:], -0.5, None, ALU.mult)
+        half_gs = [keep.tile([P, 1], F32, name="half_gs%d" % t, tag="after_h%d" % t, align_bytes=64) for t in range(PACK)]
+        for t in range(PACK):
+            nc.gpsimd.tensor_scalar(half_gs[t][:], gs_t[:, t : t + 1], -0.5, None, ALU.mult)
         cand_s_raw = gather_bytes("cand_s_raw", cand_t)
         cand_w_raw = gather_words("cand_w_raw", cand_t, "slot_b")
         cand_s = deal("cand_s", cand_s_raw, U8)
@@ -127,50 +133,63 @@ def tile_picked_twcgatebsendg_none_po_kernel(
 
         whole = slice(0, S)
         halves = [slice(0, HALF), slice(HALF, S)]
-        z_bf = keep.tile([P, S, PACK], BF16, name="z_bf", align_bytes=64)
         z_codes = keep.tile([P, S], I32, name="z_codes", align_bytes=64)
         z_scales = keep.tile([P, S], U8, name="z_scales", align_bytes=64)
         z = [keep.tile([P, 2, S], F32, name="z%d" % u) for u in range(2)]
-        d_win = [keep.tile([P, WINDOW], F32, name="d_win%d" % t) for t in range(PACK)]
-        h_win = [keep.tile([P, WINDOW], F32, name="h_win%d" % t) for t in range(PACK)]
-        gated = [keep.tile([P, S], F32, name="gated%d" % t) for t in range(PACK)]
-        other = [keep.tile([P, S], F32, name="other%d" % t) for t in range(PACK)]
+        win_slot = ["win0", "win1", "after_h0", "after_h1"]
+        gate_slot = ["gate0", "gate1", "gate2", "after_h2"]
+        d_win = {}
+        other = {}
+        gated_slot = ["gated_a", "gated_b", "gated_a", "gated_a"]
+        h_win = {}
+        gated = {}
 
         def look(lst, cols):
             return lst[:, cols.start // 16 : cols.stop // 16]
 
-        def gate_on_scalar(t):
+        def leave_d(t):
+            d_win[t] = keep.tile([P, WINDOW], F32, name="d_win%d" % t, tag=win_slot[t], align_bytes=64)
             nc.scalar.copy(d_win[t][:, :S], d_ps[t][:])
+
+        def gate_on_scalar(t):
+            other[t] = keep.tile([P, S], F32, name="other%d" % t, tag=gate_slot[t], align_bytes=64)
             nc.scalar.activation(other[t][:], d_win[t][:].indirect(n2_t[:]), ACT.Sigmoid)
 
         def half_y(t):
-            nc.scalar.activation(h_win[t][:, :S], y_ps[t][:], ACT.Copy, scale=half_gs[:, t : t + 1])
+            h_win[t] = keep.tile([P, WINDOW], F32, name="h_win%d" % t, tag=win_slot[t], align_bytes=64)
+            nc.scalar.activation(h_win[t][:, :S], y_ps[t][:], ACT.Copy, scale=half_gs[t][:])
 
         def apply_gate(t, cols):
+            if cols.start == 0:
+                gated[t] = keep.tile([P, S], F32, name="gated%d" % t, tag=gated_slot[t])
             nc.vector.scalar_tensor_tensor(gated[t][:, cols], y_ps[t][:, cols], gs_t[:, t : t + 1], other[t][:, cols], ALU.mult, ALU.mult)
 
         def mix(t, cols):
             nc.vector.tensor_tensor(z[t // 2][:, t % 2, cols], h_win[t][:].indirect(look(n1_t, cols)), gated[t][:, cols], ALU.add)
 
-        nc.scalar.activation(d_win[0][:, :S], d_ps[0][:], ACT.Sigmoid)
+        leave_d(0)
+        leave_d(1)
+        gate_on_scalar(0)
         gate_on_scalar(1)
-        nc.scalar.activation(other[0][:], y_ps[0][:], ACT.Copy, scale=gs_t[:, 0:1])
         half_y(0)
         half_y(1)
+        apply_gate(0, whole)
+        apply_gate(1, whole)
+        mix(0, whole)
+        mix(1, whole)
+        leave_d(2)
+        leave_d(3)
         gate_on_scalar(2)
         half_y(2)
         gate_on_scalar(3)
         half_y(3)
-        nc.vector.tensor_tensor(gated[0][:], d_win[0][:].indirect(n2_t[:]), other[0][:], ALU.mult)
-        apply_gate(1, whole)
-        mix(0, whole)
         apply_gate(2, whole)
-        mix(1, whole)
         mix(2, whole)
         for cols in halves:
             apply_gate(3, cols)
         for cols in halves:
             mix(3, cols)
+        z_bf = keep.tile([P, S, PACK], BF16, name="z_bf", tag="after_h3", align_bytes=64)
         lay_pair(nc.scalar.copy, z_bf, z, whole, 0)
 
         for cols in halves:
@@ -178,14 +197,13 @@ def tile_picked_twcgatebsendg_none_po_kernel(
         for cols in reversed(halves):
             nc.vector.quantize_mx(out=z_codes[:, cols].bitcast(FP8X4), scales=z_scales[:, cols], in_=z_bf[:, cols, :].rearrange("p c t -> p (c t)"))
 
-        s_win = [keep.tile([P, WINDOW], F32, name="s_win%d" % t) for t in range(PACK)]
+        s_win = [keep.tile([P, WINDOW], F32, name="s_win%d" % t, tag="s_win%d" % t) for t in range(PACK)]
         s_own = [keep.tile([P, S], F32, name="s_own%d" % t) for t in range(PACK)]
         sig = [keep.tile([P, S], F32, name="sig%d" % t) for t in range(PACK)]
-        rise = [keep.tile([P, S], F32, name="rise%d" % t) for t in range(PACK)]
+        rise = [keep.tile([P, S], F32, name="rise%d" % t, tag="rise%d" % t, align_bytes=64) for t in range(PACK)]
         lift = [keep.tile([P, S], F32, name="lift%d" % t) for t in range(PACK)]
         ds = [keep.tile([P, WINDOW], F32, name="ds%d" % t) for t in range(PACK)]
         o = [keep.tile([P, 2, S], F32, name="o%d" % u) for u in range(2)]
-        o_bf = keep.tile([P, S, PACK], BF16, name="o_bf", align_bytes=64)
         out_rows = out_0.rearrange("(p t) j -> p t j", t=PACK)
         s_ps = {}
 
@@ -209,39 +227,50 @@ def tile_picked_twcgatebsendg_none_po_kernel(
         def fetch(t):
             for u, cols in enumerate(pieces(t)):
                 nc.scalar.activation(s_win[t][:, cols], s_ps[t, u][:], ACT.Copy, scale=0.0625)
-                nc.scalar.activation(s_own[t][:, cols], s_ps[t, u][:], ACT.Copy, scale=0.0625)
+            for u, cols in enumerate(pieces(t)):
+                if t == 0 and u == 0:
+                    nc.vector.tensor_copy(s_own[t][:, cols], s_win[t][:, cols])
+                else:
+                    nc.scalar.activation(s_own[t][:, cols], s_ps[t, u][:], ACT.Copy, scale=0.0625)
             for cols in pieces(t):
-                nc.vector.tensor_tensor(rise[t][:, cols], s_win[t][:].indirect(n4_t[:, cols.start // 16 : cols.stop // 16]), s_own[t][:, cols], ALU.subtract)
+                nc.vector.tensor_tensor(rise[t][:, cols], s_win[t][:].indirect(look(n4_t, cols)), s_own[t][:, cols], ALU.subtract)
 
         def gate(t):
             nc.scalar.activation(sig[t][:], s_own[t][:], ACT.Sigmoid)
 
-        def send(t):
+        def clip(t):
             nc.scalar.activation(lift[t][:], rise[t][:], ACT.Relu)
-            nc.vector.tensor_tensor(ds[t][:].indirect(n3_t[:]), lift[t][:], s_own[t][:], ALU.add)
 
-        def finish(t, cols):
-            nc.vector.tensor_tensor(o[t // 2][:, t % 2, cols], ds[t][:, cols], sig[t][:, cols], ALU.mult)
+        def larger(engine, t, dst):
+            engine.tensor_tensor(dst, lift[t][:], s_own[t][:], ALU.add)
+
+        def send(t, src):
+            nc.vector.tensor_copy(ds[t][:].indirect(n3_t[:]), src)
+
+        def finish(engine, t, cols):
+            engine.tensor_tensor(o[t // 2][:, t % 2, cols], ds[t][:, cols], sig[t][:, cols], ALU.mult)
             nc.sync.dma_start(out_rows[:, t, cols], o[t // 2][:, t % 2, cols])
 
         for t in range(PACK):
             score(t)
         for t in range(PACK):
             fetch(t)
-        send(0)
-        send(1)
-        gate(0)
-        finish(0, whole)
-        send(2)
-        gate(1)
-        finish(1, whole)
-        gate(2)
-        finish(2, whole)
-        send(3)
+        clip(0)
+        sm_first = keep.tile([P, S], F32, name="sm_first")
+        larger(nc.vector, 0, sm_first[:])
+        send(0, sm_first[:])
+        sm_rest = keep.tile([P, PACK - 1, S], F32, name="sm_rest", tag="s_win3")
+        for t in range(1, PACK):
+            clip(t)
+            larger(nc.gpsimd, t, sm_rest[:, t - 1, :])
+            send(t, sm_rest[:, t - 1, :])
+            gate(t - 1)
+            finish(nc.gpsimd, t - 1, whole)
         gate(3)
+        o_bf = keep.tile([P, S, PACK], BF16, name="o_bf", tag="rise3", align_bytes=64)
         lay_pair(nc.scalar.copy, o_bf, o, whole, 0)
         for cols in halves:
-            finish(3, cols)
+            finish(nc.vector, 3, cols)
 
         o_codes = keep.tile([P, S], I32, name="o_codes", align_bytes=64)
         o_scales = keep.tile([P, S], U8, name="o_scales", align_bytes=64)

@@ -37,14 +37,14 @@ def tile_picked_twcgatebsendg_none_po_kernel(
 
         def load_scale_rows(queue, dst, src):
             for q in range(4):
-                queue.dma_start(dst[32 * q : 32 * q + 4, :].bitcast(I32), src[0, 4 * q : 4 * q + 4, :].bitcast(I32))
+                queue[q].dma_start(dst[32 * q : 32 * q + 4, :].bitcast(I32), src[0, 4 * q : 4 * q + 4, :].bitcast(I32))
 
         xs = keep.tile([P, T], U8, name="xs", align_bytes=64)
         ws2_raw = keep.tile([P, H], U8, name="ws2_raw", tag="slot_a", align_bytes=64)
         ws1_raw = keep.tile([P, H], U8, name="ws1_raw", tag="slot_b", align_bytes=64)
         nc.vector.memset(xs[:].bitcast(I32), 0)
         nc.vector.memset(ws2_raw[:].bitcast(I32), 0)
-        nc.vector.memset(ws1_raw[:].bitcast(I32), 0)
+        nc.gpsimd.memset(ws1_raw[:].bitcast(I32), 0)
 
         warm_in = keep.tile([P, 1], F32, name="warm_in")
         warm_out = keep.tile([P, 1], F32, name="warm_out")
@@ -59,13 +59,13 @@ def tile_picked_twcgatebsendg_none_po_kernel(
         nc.sync.dma_start(w1_raw[:].bitcast(I32), w1_words[0].bitcast(I32))
         two_t = load_list("two_t", two)
         offs_t = load_list("offs_t", offs)
-        load_scale_rows(nc.sync, xs, x_scales)
+        load_scale_rows([nc.sync] * 4, xs, x_scales)
         nc.sync.dma_start(xw[:], x_words[0].rearrange("p n t -> p (n t)").bitcast(I32))
-        load_scale_rows(nc.sync, ws2_raw, w2_scales)
+        load_scale_rows([nc.sync] * 4, ws2_raw, w2_scales)
         cand_t = load_list("cand_t", cand)
-        n2_t = load_list("n2_t", n2)
-        load_scale_rows(nc.sync, ws1_raw, w1_scales)
+        load_scale_rows([nc.gpsimd, nc.gpsimd, nc.sync, nc.sync], ws1_raw, w1_scales)
         nc.sync.dma_start(gs_t[:], gs.rearrange("(p t) o -> p (t o)", t=PACK))
+        n2_t = load_list("n2_t", n2)
         n1_t = load_list("n1_t", n1)
         n4_t = load_list("n4_t", n4)
         n3_t = load_list("n3_t", n3)
@@ -93,9 +93,9 @@ def tile_picked_twcgatebsendg_none_po_kernel(
         w2 = deal_fp4_words("w2", w2_raw)
         w1 = deal_fp4_words("w1", w1_raw)
         two_s = gather_bytes("two_s", two_t)
+        offs_s = gather_bytes("offs_s", offs_t)
         two_w = gather_words("two_w", two_t, "slot_c")
         ws2 = deal("ws2", ws2_raw, U8)
-        offs_s = gather_bytes("offs_s", offs_t)
         offs_w = gather_words("offs_w", offs_t, "slot_a")
         ws1 = deal("ws1", ws1_raw, U8)
         half_gs = [keep.tile([P, 1], F32, name="half_gs%d" % t, tag="after_h%d" % t, align_bytes=64) for t in range(PACK)]
@@ -124,8 +124,8 @@ def tile_picked_twcgatebsendg_none_po_kernel(
 
         def lay_pair(copy, dst, src, cols, pair):
             copy(
-                dst[:, cols, 2 * pair : 2 * pair + 2].rearrange("p (c i) t -> p c t i", i=4),
-                src[pair][:, :, cols].rearrange("p t (c i) -> p c t i", i=4),
+                dst[:, cols, 2 * pair : 2 * pair + 2],
+                src[pair][:, :, cols].rearrange("p t c -> p c t"),
             )
 
         def interleave(dst, src, cols):
@@ -137,10 +137,11 @@ def tile_picked_twcgatebsendg_none_po_kernel(
         z_scales = keep.tile([P, S], U8, name="z_scales", align_bytes=64)
         z = [keep.tile([P, 2, S], F32, name="z%d" % u) for u in range(2)]
         win_slot = ["win0", "win1", "after_h0", "after_h1"]
-        gate_slot = ["gate0", "gate1", "gate2", "after_h2"]
+        h_slot = ["win0", "win1", "after_h0", "after_h2"]
+        gate_slot = ["gate0", "gate1", "gate2", "after_h3"]
         d_win = {}
         other = {}
-        gated_slot = ["gated_a", "gated_b", "gated_a", "gated_a"]
+        gated_slot = ["gated_a", "gated_b", "gated_a", "gated_b"]
         h_win = {}
         gated = {}
 
@@ -153,10 +154,11 @@ def tile_picked_twcgatebsendg_none_po_kernel(
 
         def gate_on_scalar(t):
             other[t] = keep.tile([P, S], F32, name="other%d" % t, tag=gate_slot[t], align_bytes=64)
-            nc.scalar.activation(other[t][:], d_win[t][:].indirect(n2_t[:]), ACT.Sigmoid)
+            for cols in halves if t == PACK - 1 else [whole]:
+                nc.scalar.activation(other[t][:, cols], d_win[t][:].indirect(look(n2_t, cols)), ACT.Sigmoid)
 
         def half_y(t):
-            h_win[t] = keep.tile([P, WINDOW], F32, name="h_win%d" % t, tag=win_slot[t], align_bytes=64)
+            h_win[t] = keep.tile([P, WINDOW], F32, name="h_win%d" % t, tag=h_slot[t], align_bytes=64)
             nc.scalar.activation(h_win[t][:, :S], y_ps[t][:], ACT.Copy, scale=half_gs[t][:])
 
         def apply_gate(t, cols):
@@ -181,15 +183,15 @@ def tile_picked_twcgatebsendg_none_po_kernel(
         leave_d(3)
         gate_on_scalar(2)
         half_y(2)
-        gate_on_scalar(3)
         half_y(3)
+        gate_on_scalar(3)
         apply_gate(2, whole)
         mix(2, whole)
         for cols in halves:
             apply_gate(3, cols)
         for cols in halves:
             mix(3, cols)
-        z_bf = keep.tile([P, S, PACK], BF16, name="z_bf", tag="after_h3", align_bytes=64)
+        z_bf = keep.tile([P, S, PACK], BF16, name="z_bf", tag="after_h1", align_bytes=64)
         lay_pair(nc.scalar.copy, z_bf, z, whole, 0)
 
         for cols in halves:
@@ -198,14 +200,15 @@ def tile_picked_twcgatebsendg_none_po_kernel(
             nc.vector.quantize_mx(out=z_codes[:, cols].bitcast(FP8X4), scales=z_scales[:, cols], in_=z_bf[:, cols, :].rearrange("p c t -> p (c t)"))
 
         s_win = [keep.tile([P, WINDOW], F32, name="s_win%d" % t, tag="s_win%d" % t) for t in range(PACK)]
-        s_own = [keep.tile([P, S], F32, name="s_own%d" % t) for t in range(PACK)]
+        s_own = {t: keep.tile([P, S], F32, name="s_own%d" % t) for t in range(1, PACK)}
         sig = [keep.tile([P, S], F32, name="sig%d" % t) for t in range(PACK)]
         rise = [keep.tile([P, S], F32, name="rise%d" % t, tag="rise%d" % t, align_bytes=64) for t in range(PACK)]
-        lift = [keep.tile([P, S], F32, name="lift%d" % t) for t in range(PACK)]
-        ds = [keep.tile([P, WINDOW], F32, name="ds%d" % t) for t in range(PACK)]
+        lift = {t: keep.tile([P, S], F32, name="lift%d" % t) for t in range(1, PACK)}
+        ds = {}
         o = [keep.tile([P, 2, S], F32, name="o%d" % u) for u in range(2)]
         out_rows = out_0.rearrange("(p t) j -> p t j", t=PACK)
         s_ps = {}
+        sm_first = keep.tile([P, S], F32, name="sm_first")
 
         def pieces(t):
             return [halves[1], halves[0]] if t == 0 else [whole]
@@ -227,16 +230,16 @@ def tile_picked_twcgatebsendg_none_po_kernel(
         def fetch(t):
             for u, cols in enumerate(pieces(t)):
                 nc.scalar.activation(s_win[t][:, cols], s_ps[t, u][:], ACT.Copy, scale=0.0625)
-            for u, cols in enumerate(pieces(t)):
-                if t == 0 and u == 0:
-                    nc.vector.tensor_copy(s_own[t][:, cols], s_win[t][:, cols])
-                else:
-                    nc.scalar.activation(s_own[t][:, cols], s_ps[t, u][:], ACT.Copy, scale=0.0625)
-            for cols in pieces(t):
-                nc.vector.tensor_tensor(rise[t][:, cols], s_win[t][:].indirect(look(n4_t, cols)), s_own[t][:, cols], ALU.subtract)
+            if t == 0:
+                nc.vector.tensor_copy(rise[t][:], s_win[t][:].indirect(n4_t[:]))
+                for u, cols in enumerate(pieces(t)):
+                    nc.vector.scalar_tensor_tensor(sm_first[:, cols], s_ps[t, u][:], 0.0625, rise[t][:, cols], ALU.mult, ALU.max)
+            else:
+                nc.scalar.activation(s_own[t][:], s_ps[t, 0][:], ACT.Copy, scale=0.0625)
+                nc.vector.tensor_tensor(rise[t][:], s_win[t][:].indirect(n4_t[:]), s_own[t][:], ALU.subtract)
 
         def gate(t):
-            nc.scalar.activation(sig[t][:], s_own[t][:], ACT.Sigmoid)
+            nc.scalar.activation(sig[t][:], s_win[0][:, :S] if t == 0 else s_own[t][:], ACT.Sigmoid)
 
         def clip(t):
             nc.scalar.activation(lift[t][:], rise[t][:], ACT.Relu)
@@ -245,6 +248,7 @@ def tile_picked_twcgatebsendg_none_po_kernel(
             engine.tensor_tensor(dst, lift[t][:], s_own[t][:], ALU.add)
 
         def send(t, src):
+            ds[t] = keep.tile([P, WINDOW], F32, name="ds%d" % t, tag="s_win3" if t == 0 else "ds%d" % t)
             nc.vector.tensor_copy(ds[t][:].indirect(n3_t[:]), src)
 
         def finish(engine, t, cols):
@@ -255,11 +259,8 @@ def tile_picked_twcgatebsendg_none_po_kernel(
             score(t)
         for t in range(PACK):
             fetch(t)
-        clip(0)
-        sm_first = keep.tile([P, S], F32, name="sm_first")
-        larger(nc.vector, 0, sm_first[:])
         send(0, sm_first[:])
-        sm_rest = keep.tile([P, PACK - 1, S], F32, name="sm_rest", tag="s_win3")
+        sm_rest = keep.tile([P, PACK - 1, S], F32, name="sm_rest", tag="s_win2")
         for t in range(1, PACK):
             clip(t)
             larger(nc.gpsimd, t, sm_rest[:, t - 1, :])

from contextlib import ExitStack

import concourse.mybir as mybir

K, T, S, H, C = 512, 2048, 512, 512, 512
FLOPS = 3 * 2 * 512 * 512 * 512

F32 = mybir.dt.float32
BF16 = mybir.dt.bfloat16
I32 = mybir.dt.int32
U32 = mybir.dt.uint32
U16 = mybir.dt.uint16
U8 = mybir.dt.uint8
FP8X4 = mybir.dt.float8_e4m3fn_x4
FP4X4 = mybir.dt.float4_e2m1fn_x4
ALU = mybir.AluOpType
ACT = mybir.ActivationFunctionType

P = 128
PACK = 4
WINDOW = 1024
HALF = 256


def tile_picked_twcgatebsendg_none_po_kernel(
    tc, x_words, x_scales, w1_words, w1_scales, w2_words, w2_scales, gs, offs, two, n1, n2, cand, n3, n4, out_0, out_1, out_2
):
    nc = tc.nc
    with ExitStack() as ctx:
        keep = ctx.enter_context(tc.tile_pool(name="keep", bufs=1))
        psum = ctx.enter_context(tc.psum_pool(name="psum", bufs=1))

        def load_list(name, src):
            t = keep.tile([P, S // 16], U16, name=name)
            nc.sync.dma_start(t[:], src)
            return t

        def load_scale_rows(queue, dst, src):
            for q in range(4):
                queue[q].dma_start(dst[32 * q : 32 * q + 4, :].bitcast(I32), src[0, 4 * q : 4 * q + 4, :].bitcast(I32))

        xs = keep.tile([P, T], U8, name="xs", align_bytes=64)
        ws2_raw = keep.tile([P, H], U8, name="ws2_raw", tag="slot_a", align_bytes=64)
        ws1_raw = keep.tile([P, H], U8, name="ws1_raw", tag="slot_b", align_bytes=64)
        nc.vector.memset(xs[:].bitcast(I32), 0)
        nc.vector.memset(ws2_raw[:].bitcast(I32), 0)
        nc.gpsimd.memset(ws1_raw[:].bitcast(I32), 0)

        warm_in = keep.tile([P, 1], F32, name="warm_in")
        warm_out = keep.tile([P, 1], F32, name="warm_out")
        nc.gpsimd.memset(warm_in[:], 0.0)
        nc.scalar.activation(warm_out[:], warm_in[:], ACT.Sigmoid)

        w2_raw = keep.tile([P, 2 * H], U8, name="w2_raw", align_bytes=64)
        w1_raw = keep.tile([P, 2 * H], U8, name="w1_raw", align_bytes=64)
        xw = keep.tile([P, T], I32, name="xw", align_bytes=64)
        gs_t = keep.tile([P, PACK], F32, name="gs_t")
        nc.sync.dma_start(w2_raw[:].bitcast(I32), w2_words[0].bitcast(I32))
        nc.sync.dma_start(w1_raw[:].bitcast(I32), w1_words[0].bitcast(I32))
        two_t = load_list("two_t", two)
        offs_t = load_list("offs_t", offs)
        load_scale_rows([nc.sync] * 4, xs, x_scales)
        nc.sync.dma_start(xw[:], x_words[0].rearrange("p n t -> p (n t)").bitcast(I32))
        load_scale_rows([nc.sync] * 4, ws2_raw, w2_scales)
        cand_t = load_list("cand_t", cand)
        load_scale_rows([nc.gpsimd, nc.gpsimd, nc.sync, nc.sync], ws1_raw, w1_scales)
        nc.sync.dma_start(gs_t[:], gs.rearrange("(p t) o -> p (t o)", t=PACK))
        n2_t = load_list("n2_t", n2)
        n1_t = load_list("n1_t", n1)
        n4_t = load_list("n4_t", n4)
        n3_t = load_list("n3_t", n3)

        def deal_fp4_words(name, raw):
            d = keep.tile([P, 2 * H], U8, name=name, align_bytes=64)
            nc.vector.tensor_copy(d[:].rearrange("p (t m b) -> p t m b", t=PACK, b=2), raw[:].rearrange("p (m t b) -> p t m b", t=PACK, b=2))
            return d

        def deal(name, raw, dtype):
            d = keep.tile([P, S], dtype, name=name, align_bytes=64)
            nc.vector.tensor_copy(d[:].rearrange("p (t m) -> p t m", t=PACK), raw[:].rearrange("p (m t) -> p t m", t=PACK))
            return d

        def gather_words(name, lst, slot):
            g = keep.tile([P, S], I32, name=name, tag=slot, align_bytes=64)
            nc.vector.tensor_copy(g[:].bitcast(U32), xw[:].bitcast(U32).indirect(lst[:]))
            return g

        def gather_bytes(name, lst):
            g = keep.tile([P, S], U8, name=name, align_bytes=64)
            nc.vector.tensor_copy(g[:], xs[:].indirect(lst[:]))
            return g

        w2 = deal_fp4_words("w2", w2_raw)
        w1 = deal_fp4_words("w1", w1_raw)
        two_s = gather_bytes("two_s", two_t)
        offs_s = gather_bytes("offs_s", offs_t)
        two_w = gather_words("two_w", two_t, "slot_c")
        ws2 = deal("ws2", ws2_raw, U8)
        offs_w = gather_words("offs_w", offs_t, "slot_a")
        ws1 = deal("ws1", ws1_raw, U8)
        half_gs = [keep.tile([P, 1], F32, name="half_gs%d" % t, tag="after_h%d" % t, align_bytes=64) for t in range(PACK)]
        for t in range(PACK):
            nc.gpsimd.tensor_scalar(half_gs[t][:], gs_t[:, t : t + 1], -0.5, None, ALU.mult)
        cand_s_raw = gather_bytes("cand_s_raw", cand_t)
        cand_w_raw = gather_words("cand_w_raw", cand_t, "slot_b")
        cand_s = deal("cand_s", cand_s_raw, U8)
        cand_w = deal("cand_w", cand_w_raw, I32)

        def project(bank, w, ws, xg, xgs, t):
            acc = psum.tile([P, S], F32, name="acc", tag="bank%d" % bank)
            nc.tensor.matmul_mx(
                out=acc[:],
                lhsT=w[:, 2 * P * t : 2 * P * (t + 1)].bitcast(FP4X4),
                lhsT_scale=ws[:, P * t : P * (t + 1)],
                rhs=xg[:].bitcast(FP8X4),
                rhs_scale=xgs[:],
                start=True,
                stop=True,
            )
            return acc

        d_ps = [project(t, w2, ws2, two_w, two_s, t) for t in range(PACK)]
        y_ps = [project(PACK + t, w1, ws1, offs_w, offs_s, t) for t in range(PACK)]

        def lay_pair(copy, dst, src, cols, pair):
            copy(
                dst[:, cols, 2 * pair : 2 * pair + 2],
                src[pair][:, :, cols].rearrange("p t c -> p c t"),
            )

        def interleave(dst, src, cols):
            lay_pair(nc.scalar.copy if cols.start == 0 else nc.vector.tensor_copy, dst, src, cols, 1)

        whole = slice(0, S)
        halves = [slice(0, HALF), slice(HALF, S)]
        z_codes = keep.tile([P, S], I32, name="z_codes", align_bytes=64)
        z_scales = keep.tile([P, S], U8, name="z_scales", align_bytes=64)
        z = [keep.tile([P, 2, S], F32, name="z%d" % u) for u in range(2)]
        win_slot = ["win0", "win1", "after_h0", "after_h1"]
        h_slot = ["win0", "win1", "after_h0", "after_h2"]
        gate_slot = ["gate0", "gate1", "gate2", "after_h3"]
        d_win = {}
        other = {}
        gated_slot = ["gated_a", "gated_b", "gated_a", "gated_b"]
        h_win = {}
        gated = {}

        def look(lst, cols):
            return lst[:, cols.start // 16 : cols.stop // 16]

        def leave_d(t):
            d_win[t] = keep.tile([P, WINDOW], F32, name="d_win%d" % t, tag=win_slot[t], align_bytes=64)
            nc.scalar.copy(d_win[t][:, :S], d_ps[t][:])

        def gate_on_scalar(t):
            other[t] = keep.tile([P, S], F32, name="other%d" % t, tag=gate_slot[t], align_bytes=64)
            for cols in halves if t == PACK - 1 else [whole]:
                nc.scalar.activation(other[t][:, cols], d_win[t][:].indirect(look(n2_t, cols)), ACT.Sigmoid)

        def half_y(t):
            h_win[t] = keep.tile([P, WINDOW], F32, name="h_win%d" % t, tag=h_slot[t], align_bytes=64)
            nc.scalar.activation(h_win[t][:, :S], y_ps[t][:], ACT.Copy, scale=half_gs[t][:])

        def apply_gate(t, cols):
            if cols.start == 0:
                gated[t] = keep.tile([P, S], F32, name="gated%d" % t, tag=gated_slot[t])
            nc.vector.scalar_tensor_tensor(gated[t][:, cols], y_ps[t][:, cols], gs_t[:, t : t + 1], other[t][:, cols], ALU.mult, ALU.mult)

        def mix(t, cols):
            nc.vector.tensor_tensor(z[t // 2][:, t % 2, cols], h_win[t][:].indirect(look(n1_t, cols)), gated[t][:, cols], ALU.add)

        leave_d(0)
        leave_d(1)
        gate_on_scalar(0)
        gate_on_scalar(1)
        half_y(0)
        half_y(1)
        apply_gate(0, whole)
        apply_gate(1, whole)
        mix(0, whole)
        mix(1, whole)
        leave_d(2)
        leave_d(3)
        gate_on_scalar(2)
        half_y(2)
        half_y(3)
        gate_on_scalar(3)
        apply_gate(2, whole)
        mix(2, whole)
        for cols in halves:
            apply_gate(3, cols)
        for cols in halves:
            mix(3, cols)
        z_bf = keep.tile([P, S, PACK], BF16, name="z_bf", tag="after_h1", align_bytes=64)
        lay_pair(nc.scalar.copy, z_bf, z, whole, 0)

        for cols in halves:
            interleave(z_bf, z, cols)
        for cols in reversed(halves):
            nc.vector.quantize_mx(out=z_codes[:, cols].bitcast(FP8X4), scales=z_scales[:, cols], in_=z_bf[:, cols, :].rearrange("p c t -> p (c t)"))

        s_win = [keep.tile([P, WINDOW], F32, name="s_win%d" % t, tag="s_win%d" % t) for t in range(PACK)]
        s_own = {t: keep.tile([P, S], F32, name="s_own%d" % t) for t in range(1, PACK)}
        sig = [keep.tile([P, S], F32, name="sig%d" % t) for t in range(PACK)]
        rise = [keep.tile([P, S], F32, name="rise%d" % t, tag="rise%d" % t, align_bytes=64) for t in range(PACK)]
        lift = {t: keep.tile([P, S], F32, name="lift%d" % t) for t in range(1, PACK)}
        ds = {}
        o = [keep.tile([P, 2, S], F32, name="o%d" % u) for u in range(2)]
        out_rows = out_0.rearrange("(p t) j -> p t j", t=PACK)
        s_ps = {}
        sm_first = keep.tile([P, S], F32, name="sm_first")

        def pieces(t):
            return [halves[1], halves[0]] if t == 0 else [whole]

        def score(t):
            for u, cols in enumerate(pieces(t)):
                acc = psum.tile([P, cols.stop - cols.start], F32, name="acc", tag="bank%d" % (t + PACK * u))
                nc.tensor.matmul_mx(
                    out=acc[:],
                    lhsT=cand_w[:, P * t : P * (t + 1)].bitcast(FP8X4),
                    lhsT_scale=cand_s[:, P * t : P * (t + 1)],
                    rhs=z_codes[:, cols].bitcast(FP8X4),
                    rhs_scale=z_scales[:, cols],
                    start=True,
                    stop=True,
                )
                s_ps[t, u] = acc

        def fetch(t):
            for u, cols in enumerate(pieces(t)):
                nc.scalar.activation(s_win[t][:, cols], s_ps[t, u][:], ACT.Copy, scale=0.0625)
            if t == 0:
                nc.vector.tensor_copy(rise[t][:], s_win[t][:].indirect(n4_t[:]))
                for u, cols in enumerate(pieces(t)):
                    nc.vector.scalar_tensor_tensor(sm_first[:, cols], s_ps[t, u][:], 0.0625, rise[t][:, cols], ALU.mult, ALU.max)
            else:
                nc.scalar.activation(s_own[t][:], s_ps[t, 0][:], ACT.Copy, scale=0.0625)
                nc.vector.tensor_tensor(rise[t][:], s_win[t][:].indirect(n4_t[:]), s_own[t][:], ALU.subtract)

        def gate(t):
            nc.scalar.activation(sig[t][:], s_win[0][:, :S] if t == 0 else s_own[t][:], ACT.Sigmoid)

        def clip(t):
            nc.scalar.activation(lift[t][:], rise[t][:], ACT.Relu)

        def larger(engine, t, dst):
            engine.tensor_tensor(dst, lift[t][:], s_own[t][:], ALU.add)

        def send(t, src):
            ds[t] = keep.tile([P, WINDOW], F32, name="ds%d" % t, tag="s_win3" if t == 0 else "ds%d" % t)
            nc.vector.tensor_copy(ds[t][:].indirect(n3_t[:]), src)

        def finish(engine, t, cols):
            engine.tensor_tensor(o[t // 2][:, t % 2, cols], ds[t][:, cols], sig[t][:, cols], ALU.mult)
            nc.sync.dma_start(out_rows[:, t, cols], o[t // 2][:, t % 2, cols])

        for t in range(PACK):
            score(t)
        for t in range(PACK):
            fetch(t)
        send(0, sm_first[:])
        sm_rest = keep.tile([P, PACK - 1, S], F32, name="sm_rest", tag="s_win2")
        for t in range(1, PACK):
            clip(t)
            larger(nc.gpsimd, t, sm_rest[:, t - 1, :])
            send(t, sm_rest[:, t - 1, :])
            gate(t - 1)
            finish(nc.gpsimd, t - 1, whole)
        gate(3)
        o_bf = keep.tile([P, S, PACK], BF16, name="o_bf", tag="rise3", align_bytes=64)
        lay_pair(nc.scalar.copy, o_bf, o, whole, 0)
        for cols in halves:
            finish(nc.vector, 3, cols)

        o_codes = keep.tile([P, S], I32, name="o_codes", align_bytes=64)
        o_scales = keep.tile([P, S], U8, name="o_scales", align_bytes=64)
        for cols in halves:
            interleave(o_bf, o, cols)
        words_out = out_1[0].rearrange("p n t -> p (n t)").bitcast(I32)
        for cols in reversed(halves):
            nc.vector.quantize_mx(out=o_codes[:, cols].bitcast(FP8X4), scales=o_scales[:, cols], in_=o_bf[:, cols, :].rearrange("p c t -> p (c t)"))
            nc.scalar.dma_start(words_out[:, cols], o_codes[:, cols])
        for q in range(4):
            eng = nc.sync if q % 2 == 0 else nc.scalar
            eng.dma_start(out_2[0, 4 * q : 4 * q + 4, :].bitcast(I32), o_scales[32 * q : 32 * q + 4, :].bitcast(I32))
